import numpy as np
import ml_dtypes


def mxq(x, axis, fmt="e4m3"):
    dtype, down = {"e4m3": (ml_dtypes.float8_e4m3fn, 7), "e5m2": (ml_dtypes.float8_e5m2, 14)}[fmt]
    v = np.moveaxis(np.asarray(x, np.float32).astype(ml_dtypes.bfloat16).astype(np.float64), axis, -1)
    blocks = v.reshape(v.shape[:-1] + (-1, 32))
    amax = np.abs(blocks).max(-1, keepdims=True)
    byte = np.maximum(np.where(amax > 0, np.frexp(amax)[1] - 1 + 127, 0) - down, 1)
    scale = np.exp2(byte - 127.0)
    codes = (blocks / scale).astype(np.float32).astype(dtype).astype(np.float64)
    return np.moveaxis((codes * scale).reshape(v.shape), -1, axis)


WIDE = False


def mx_kscale(k):
    if not WIDE:
        return np.ones(k)
    levels = np.array([10, -10, 5, -5, 0])
    if k % 512:
        return np.exp2(np.random.permutation(np.resize(levels, k // 32))).repeat(32)
    a = np.empty((k // 512, 16))
    for p in range(k // 512):
        a[p, :8] = np.random.permutation(np.resize(levels, 8))
        for g in range(8):
            far = levels[np.abs(levels - a[p, g]) >= 10]
            a[p, g + 8] = far[np.random.randint(len(far))]
    return np.exp2(a.ravel()).repeat(32)


def f64(x):
    return np.asarray(x).astype(np.float64)


E2M1 = np.array([0.0, 0.5, 1.0, 1.5, 2.0, 3.0, 4.0, 6.0, -0.0, -0.5, -1.0, -1.5, -2.0, -3.0, -4.0, -6.0])


def pack_weight(w, fmt):
    k, n = w.shape
    w = f64(np.asarray(w, np.float32).astype(ml_dtypes.bfloat16)).reshape(k // 32, 32, n)
    amax = np.abs(w).max(1)
    if fmt == "e4m3":
        byte = np.frexp(amax)[1] - 1 + 127 - 7
    else:
        mant, ex = np.frexp(amax / 6.0)
        byte = np.where(mant > 0.5, ex, ex - 1) + 127
    byte = np.clip(np.where(amax > 0, byte, 1), 1, 254)
    scaled = (w * np.exp2(127.0 - byte)[:, None, :]).reshape(k, n).astype(np.float32)
    by_word = np.ascontiguousarray(scaled.reshape(k // 512, 128, 4, n).transpose(0, 1, 3, 2))
    if fmt == "e4m3":
        words = by_word.astype(ml_dtypes.float8_e4m3fn).view(np.uint8)
    else:
        c = by_word.astype(ml_dtypes.float4_e2m1fn).view(np.uint8) & 0xF
        words = (c[..., 0::2] | (c[..., 1::2] << 4)).reshape(k // 512, 128, 2 * n)
    return np.ascontiguousarray(words), np.ascontiguousarray(byte.astype(np.uint8).reshape(k // 512, 16, n))


def unpack_weight(words, scales, fmt):
    g, _, n = scales.shape
    words = np.ascontiguousarray(words).reshape(g, 128, n, -1)
    if fmt == "e4m3":
        vals = words.view(ml_dtypes.float8_e4m3fn).astype(np.float64)
    else:
        nib = np.empty((g, 128, n, 4), np.uint8)
        nib[..., 0::2] = words & 0xF
        nib[..., 1::2] = words >> 4
        vals = E2M1[nib]
    vals = vals * np.repeat(np.exp2(scales.astype(np.float64) - 127.0), 8, axis=1)[..., None]
    return vals.transpose(0, 1, 3, 2).reshape(g * 512, n)


def planes(y):
    n, m = y.shape
    v = y.astype(np.float32).astype(ml_dtypes.bfloat16).astype(np.float64).reshape(n // 32, 32, m)
    top = np.abs(v).max(1)
    byte = np.clip(np.where(top > 0, np.frexp(top)[1] - 1 + 127 - 7, 1), 1, 254)
    codes = (v * np.exp2(127.0 - byte)[:, None, :]).reshape(n, m).astype(np.float32).astype(ml_dtypes.float8_e4m3fn).view(np.uint8)
    words = codes.reshape(n // 512, 128, 4, m).transpose(0, 1, 3, 2)
    return np.ascontiguousarray(words), np.ascontiguousarray(byte.astype(np.uint8).reshape(n // 512, 16, m))


O, K, M, T = 512, 1024, 2048, 1024


def setup_inputs():
    n = np.random.standard_normal
    s = mx_kscale(K)[:, None]
    x = n((K, T)); x[:O] *= 6.0
    w = n((K, M)) / np.sqrt(K) / s; w[:O] /= 2.0
    p_w8 = pack_weight(w[:O], "e4m3")
    p_w4 = pack_weight(w[O:], "e2m1")
    return {
        "x": (x * s).astype(np.float32),
        "w8_words": p_w8[0],
        "w8_scales": p_w8[1],
        "w4_words": p_w4[0],
        "w4_scales": p_w4[1],
    }


def reference(x, w8_words, w8_scales, w4_words, w4_scales):
    x_ = mxq(f64(x), 0, "e4m3")
    w8_ = unpack_weight(w8_words, w8_scales, "e4m3")
    w4_ = unpack_weight(w4_words, w4_scales, "e2m1")
    y = w8_.T @ x_[:O] + w4_.T @ x_[O:]
    out_0 = np.maximum(y, 0.0) ** 2
    return (out_0,) + planes(out_0)

@@ -1,0 +1,269 @@
+from contextlib import ExitStack
+
+import concourse.mybir as mybir
+
+K, M, T = 1024, 2048, 1024
+FLOPS = 2 * K * M * T
+
+F32 = mybir.dt.float32
+BF16 = mybir.dt.bfloat16
+I32 = mybir.dt.int32
+U32 = mybir.dt.uint32
+U8 = mybir.dt.uint8
+FP8X4 = mybir.dt.float8_e4m3fn_x4
+FP4X4 = mybir.dt.float4_e2m1fn_x4
+ACT = mybir.ActivationFunctionType
+ALU = mybir.AluOpType
+
+P = 128
+HALF = 512
+QUARTER = 256
+BLOCKS = 4
+UNITS = 8
+VECTOR_BANKS = [0, 0, 0, 2, 2, 2, 2, 2]
+
+
+def tile_mix_outl_fm_pl_relu2_kernel(tc, x, w8_words, w8_scales, w4_words, w4_scales, out_0, out_1, out_2):
+    nc = tc.nc
+    w8_bytes = w8_words[0].rearrange("p n i -> p (n i)")
+    w4_bytes = w4_words[0]
+
+    with ExitStack() as ctx:
+        sb = ctx.enter_context(tc.tile_pool(name="sb", bufs=1))
+        psum = ctx.enter_context(tc.psum_pool(name="psum", bufs=1))
+        ctx.enter_context(tc.manual_schedule())
+
+        def sbuf(name, shape, dtype):
+            return sb.tile(shape, dtype, name=name, align_bytes=64)
+
+        scale_raw = sbuf("scale_raw", [P, M], U8)
+        out_scales = sbuf("out_scales", [P, T], U8)
+        x_codes = {(g, h): sbuf("x_codes_%d_%d" % (g, h), [P, HALF], U32) for g in range(2) for h in range(2)}
+        x_scales = {(g, h): sbuf("x_scales_%d_%d" % (g, h), [P, HALF], U8) for g in range(2) for h in range(2)}
+        x_raw, x_bf, w8_raw, w4_raw, w8, w4, w_scales = {}, {}, {}, {}, {}, {}, {}
+        banks, result, result_bf, words = {}, {}, {}, {}
+
+        def load_x(g, t0, width):
+            x_raw[g, t0] = sbuf("x_raw_%d_%d" % (g, t0), [P, 4, width], F32)
+            nc.sync.dma_start(out=x_raw[g, t0][:], in_=x[512 * g : 512 * (g + 1), t0 : t0 + width].rearrange("(p j) w -> p j w", j=4))
+
+        def load_w8(a, count):
+            raw = sbuf("w8_raw_%d" % a, [P, 512 * count], I32)
+            nc.sync.dma_start(out=raw[:], in_=w8_bytes[:, 2048 * a : 2048 * (a + count)].bitcast(I32))
+            for i in range(count):
+                w8_raw[a + i] = raw[:, 512 * i : 512 * (i + 1)]
+
+        def load_w4(a, count):
+            raw = sbuf("w4_raw_%d" % a, [P, 1024 * count], U8)
+            nc.sync.dma_start(out=raw[:].bitcast(I32), in_=w4_bytes[:, 1024 * a : 1024 * (a + count)].bitcast(I32))
+            for i in range(count):
+                w4_raw[a + i] = raw[:, 1024 * i : 1024 * (i + 1)]
+
+        def load_scales(queue, scales, first_row):
+            for q in range(4):
+                row = 32 * q + first_row
+                queue.dma_start(out=scale_raw[row : row + 4, :].bitcast(I32), in_=scales[0, 4 * q : 4 * q + 4, :].bitcast(I32))
+
+        def deal_w8(a):
+            w8[a] = sbuf("w8_%d" % a, [P, 512], U32)
+            nc.vector.tensor_copy(
+                out=w8[a][:].bitcast(I32).rearrange("p (r h l) -> p h r l", r=4, l=4),
+                in_=w8_raw[a].rearrange("p (h l r) -> p h r l", r=4, l=4),
+            )
+
+        def deal_w4(a):
+            w4[a] = sbuf("w4_%d" % a, [P, 1024], U8)
+            nc.vector.tensor_copy(
+                out=w4[a][:].rearrange("p (r h l b) -> p h r l b", r=4, l=8, b=2),
+                in_=w4_raw[a].rearrange("p (h l r b) -> p h r l b", r=4, l=8, b=2),
+            )
+
+        def deal_scales(a):
+            w_scales[a] = sbuf("w_scales_%d" % a, [P, 512], U8)
+            nc.vector.tensor_copy(
+                out=w_scales[a][:].rearrange("p (r h l) -> p h r l", r=4, l=16),
+                in_=scale_raw[:, 512 * a : 512 * (a + 1)].rearrange("p (h l r) -> p h r l", r=4, l=16),
+            )
+
+        def interleave(on_scalar, dst, src):
+            out = dst.rearrange("p (c i j) -> p c j i", i=4, j=4)
+            in_ = src.rearrange("p j (c i) -> p c j i", i=4)
+            if on_scalar:
+                nc.scalar.activation(out=out, in_=in_, func=ACT.Copy)
+            else:
+                nc.vector.tensor_copy(out=out, in_=in_)
+
+        def round_x(on_scalar, g, t0):
+            width = x_raw[g, t0].shape[2]
+            x_bf[g, t0] = sbuf("x_bf_%d_%d" % (g, t0), [P, 4 * width], BF16)
+            interleave(on_scalar, x_bf[g, t0][:], x_raw[g, t0][:])
+
+        def quantize_x(g, t0):
+            width = x_raw[g, t0].shape[2]
+            h, c0 = divmod(t0, HALF)
+            nc.vector.quantize_mx(
+                out=x_codes[g, h][:, c0 : c0 + width].bitcast(FP8X4),
+                scales=x_scales[g, h][:, c0 : c0 + width],
+                in_=x_bf[g, t0][:],
+            )
+
+        def pass_w8(out, a, r, h, c0, width, start):
+            nc.tensor.matmul_mx(
+                out=out,
+                lhsT=w8[a][:, P * r : P * (r + 1)].bitcast(FP8X4),
+                lhsT_scale=w_scales[a][4:P, P * r : P * (r + 1)],
+                rhs=x_codes[0, h][:, c0 : c0 + width].bitcast(FP8X4),
+                rhs_scale=x_scales[0, h][:, c0 : c0 + width],
+                start=start,
+                stop=False,
+            )
+
+        def pass_w4(out, a, r, h, c0, width, stop):
+            nc.tensor.matmul_mx(
+                out=out,
+                lhsT=w4[a][:, 2 * P * r : 2 * P * (r + 1)].bitcast(FP4X4),
+                lhsT_scale=w_scales[a][:, P * r : P * (r + 1)],
+                rhs=x_codes[1, h][:, c0 : c0 + width].bitcast(FP8X4),
+                rhs_scale=x_scales[1, h][:, c0 : c0 + width],
+                start=False,
+                stop=stop,
+            )
+
+        def first_w8(c):
+            for b in range(2):
+                banks[c, b, "q"] = psum.tile([P, 2, QUARTER], F32, name="q_%d_%d" % (c, b), tag="bank%d" % (2 * c + b))
+                for i in range(2):
+                    pass_w8(banks[c, b, "q"][:, i, :], 0, 2 * b + i, 0, QUARTER * c, QUARTER, i == 0)
+
+        def first_w4(c):
+            for b in range(2):
+                for i in range(2):
+                    for n in range(2):
+                        pass_w4(banks[c, b, "q"][:, i, P * n : P * (n + 1)], 0, 2 * b + i, 0, QUARTER * c + P * n, P, i == 1 and n == 1)
+
+        def first_epilogue(c):
+            cols = slice(QUARTER * c, QUARTER * (c + 1))
+            for b in range(2):
+                nc.scalar.activation(out=result[0][:, 2 * b : 2 * b + 2, cols], in_=banks[c, b, "q"][:], func=ACT.Relu)
+            nc.scalar.activation(out=result[0][:, :, cols], in_=result[0][:, :, cols], func=ACT.Square)
+
+        def multiply(u, r):
+            h, a = divmod(u, BLOCKS)
+            banks[u, r] = psum.tile([P, HALF], F32, name="acc_%d_%d" % (u, r), tag="bank%d" % (4 * (u % 2) + r))
+            pass_w8(banks[u, r][:], a, r, h, 0, HALF, True)
+            pass_w4(banks[u, r][:], a, r, h, 0, HALF, True)
+
+        def new_result(u):
+            result[u] = sbuf("result_%d" % u, [P, 4, HALF], F32)
+
+        def relu_vector(u, r):
+            nc.vector.tensor_scalar_max(out=result[u][:, r, :], in0=banks[u, r][:], scalar1=0.0)
+
+        def relu_scalar(u, r):
+            nc.scalar.activation(out=result[u][:, r, :], in_=banks[u, r][:], func=ACT.Relu)
+
+        def square(u, r0):
+            rows = result[u][:, r0 : r0 + 2, :]
+            nc.scalar.activation(out=rows, in_=rows, func=ACT.Square)
+
+        def store_result(u, r0):
+            h, a = divmod(u, BLOCKS)
+            dst = out_0[512 * a : 512 * (a + 1), HALF * h : HALF * (h + 1)].rearrange("(p r) t -> p r t", r=4)
+            nc.sync.dma_start(out=dst[:, r0 : r0 + 2, :], in_=result[u][:, r0 : r0 + 2, :])
+
+        def round_result(u):
+            result_bf[u] = sb.tile([P, 4 * HALF], BF16, name="result_bf_%d" % u, tag="result_bf", bufs=2, align_bytes=64)
+            interleave(False, result_bf[u][:], result[u][:])
+
+        def quantize_result(u):
+            h, a = divmod(u, BLOCKS)
+            words[u] = sbuf("words_%d" % u, [P, HALF], U32)
+            nc.vector.quantize_mx(
+                out=words[u][:].bitcast(FP8X4),
+                scales=out_scales[4 * a : P, HALF * h : HALF * (h + 1)],
+                in_=result_bf[u][:],
+            )
+
+        def store_words(u):
+            h, a = divmod(u, BLOCKS)
+            dst = out_1[a].rearrange("p t i -> p (t i)")[:, 4 * HALF * h : 4 * HALF * (h + 1)]
+            nc.sync.dma_start(out=dst.bitcast(I32), in_=words[u][:].bitcast(I32))
+
+        nc.vector.memset(scale_raw[:].bitcast(I32), 0)
+        load_x(0, 0, QUARTER)
+        load_scales(nc.sync, w8_scales, 4)
+        load_w8(0, 1)
+        load_w4(0, 1)
+        load_x(1, 0, QUARTER)
+        load_scales(nc.sync, w4_scales, 0)
+        load_x(0, QUARTER, QUARTER)
+        load_w8(1, 1)
+        load_x(1, QUARTER, QUARTER)
+        load_w4(1, 1)
+        load_w8(2, 2)
+        load_w4(2, 2)
+        load_x(0, HALF, HALF)
+        load_x(1, HALF, HALF)
+
+        new_result(0)
+        round_x(True, 0, 0)
+        deal_w8(0)
+        deal_w4(0)
+        quantize_x(0, 0)
+        round_x(False, 1, 0)
+        deal_scales(0)
+        first_w8(0)
+        quantize_x(1, 0)
+        first_w4(0)
+        round_x(True, 0, QUARTER)
+        round_x(False, 1, QUARTER)
+        quantize_x(0, QUARTER)
+        first_w8(1)
+        deal_w8(1)
+        quantize_x(1, QUARTER)
+        first_w4(1)
+        first_epilogue(0)
+        first_epilogue(1)
+        store_result(0, 0)
+        store_result(0, 2)
+        deal_w4(1)
+        deal_scales(1)
+        for a in (2, 3):
+            deal_w8(a)
+            deal_w4(a)
+            deal_scales(a)
+
+        def extra(u, slot):
+            if u == 1 and slot == 0:
+                round_x(False, 0, HALF)
+            if u == 1 and slot == 1:
+                round_x(False, 1, HALF)
+                quantize_x(0, HALF)
+            if u == 2 and slot == 0:
+                quantize_x(1, HALF)
+            if u + 1 < UNITS and slot < VECTOR_BANKS[u + 1]:
+                multiply(u + 1, slot)
+                relu_vector(u + 1, slot)
+
+        new_result(1)
+        for u in range(1, UNITS):
+            if u + 1 < UNITS:
+                new_result(u + 1)
+            for r in range(VECTOR_BANKS[u], 4):
+                multiply(u, r)
+                relu_scalar(u, r)
+            round_result(u - 1)
+            extra(u, 0)
+            quantize_result(u - 1)
+            extra(u, 1)
+            square(u, 0)
+            store_result(u, 0)
+            store_words(u - 1)
+            square(u, 2)
+            store_result(u, 2)
+        round_result(UNITS - 1)
+        quantize_result(UNITS - 1)
+        store_words(UNITS - 1)
+        for q in range(4):
+            queue = nc.sync if q % 2 else nc.scalar
+            queue.dma_start(out=out_2[:, 4 * q : 4 * q + 4, :].bitcast(I32), in_=out_scales[32 * q : 32 * q + 16, :].bitcast(I32))

@@ -20,7 +20,7 @@ HALF = 512
 QUARTER = 256
 BLOCKS = 4
 UNITS = 8
-VECTOR_BANKS = [0, 0, 0, 2, 2, 2, 2, 2]
+VECTOR_BANKS = [0,0,0,1,2,2,2,2]
 
 
 def tile_mix_outl_fm_pl_relu2_kernel(tc, x, w8_words, w8_scales, w4_words, w4_scales, out_0, out_1, out_2):
@@ -129,23 +129,23 @@ def tile_mix_outl_fm_pl_relu2_kernel(tc, x, w8_words, w8_scales, w4_words, w4_sc
                 stop=stop,
             )
 
-        def first_w8(c):
-            for b in range(2):
-                banks[c, b, "q"] = psum.tile([P, 2, QUARTER], F32, name="q_%d_%d" % (c, b), tag="bank%d" % (2 * c + b))
-                for i in range(2):
-                    pass_w8(banks[c, b, "q"][:, i, :], 0, 2 * b + i, 0, QUARTER * c, QUARTER, i == 0)
+        def quarter_bank(a, c, b, on_scalar):
+            bank = psum.tile([P, 2, QUARTER], F32, name="q_%d_%d_%d" % (a, c, b), tag="bank%d" % (4 * c + 2 * a + b))
+            for i in range(2):
+                pass_w8(bank[:, i, :], a, 2 * b + i, 0, QUARTER * c, QUARTER, i == 0)
+            for i in range(2):
+                for n in range(2):
+                    pass_w4(bank[:, i, P * n : P * (n + 1)], a, 2 * b + i, 0, QUARTER * c + P * n, P, i == 1 and n == 1)
+            out = result[a][:, 2 * b : 2 * b + 2, QUARTER * c : QUARTER * (c + 1)]
+            if on_scalar:
+                nc.scalar.activation(out=out, in_=bank[:], func=ACT.Relu)
+            else:
+                nc.vector.tensor_scalar_max(out=out, in0=bank[:], scalar1=0.0)
 
-        def first_w4(c):
-            for b in range(2):
-                for i in range(2):
-                    for n in range(2):
-                        pass_w4(banks[c, b, "q"][:, i, P * n : P * (n + 1)], 0, 2 * b + i, 0, QUARTER * c + P * n, P, i == 1 and n == 1)
-
-        def first_epilogue(c):
-            cols = slice(QUARTER * c, QUARTER * (c + 1))
-            for b in range(2):
-                nc.scalar.activation(out=result[0][:, 2 * b : 2 * b + 2, cols], in_=banks[c, b, "q"][:], func=ACT.Relu)
-            nc.scalar.activation(out=result[0][:, :, cols], in_=result[0][:, :, cols], func=ACT.Square)
+        def quarter_square(a, c):
+            part = result[a][:, :, QUARTER * c : QUARTER * (c + 1)]
+            nc.scalar.activation(out=part, in_=part, func=ACT.Square)
+            store_result(a, 0, 4, QUARTER * c, QUARTER)
 
         def multiply(u, r):
             h, a = divmod(u, BLOCKS)
@@ -166,10 +166,10 @@ def tile_mix_outl_fm_pl_relu2_kernel(tc, x, w8_words, w8_scales, w4_words, w4_sc
             rows = result[u][:, r0 : r0 + 2, :]
             nc.scalar.activation(out=rows, in_=rows, func=ACT.Square)
 
-        def store_result(u, r0):
+        def store_result(u, r0, rows=2, c0=0, width=HALF):
             h, a = divmod(u, BLOCKS)
-            dst = out_0[512 * a : 512 * (a + 1), HALF * h : HALF * (h + 1)].rearrange("(p r) t -> p r t", r=4)
-            nc.sync.dma_start(out=dst[:, r0 : r0 + 2, :], in_=result[u][:, r0 : r0 + 2, :])
+            dst = out_0[512 * a : 512 * (a + 1), HALF * h + c0 : HALF * h + c0 + width].rearrange("(p r) t -> p r t", r=4)
+            nc.sync.dma_start(out=dst[:, r0 : r0 + rows, :], in_=result[u][:, r0 : r0 + rows, c0 : c0 + width])
 
         def round_result(u):
             result_bf[u] = sb.tile([P, 4 * HALF], BF16, name="result_bf_%d" % u, tag="result_bf", bufs=2, align_bytes=64)
@@ -184,6 +184,10 @@ def tile_mix_outl_fm_pl_relu2_kernel(tc, x, w8_words, w8_scales, w4_words, w4_sc
                 in_=result_bf[u][:],
             )
 
+        def square_cols(u, r, c0, width):
+            rows = result[u][:, r, c0 : c0 + width]
+            nc.scalar.activation(out=rows, in_=rows, func=ACT.Square)
+
         def store_words(u):
             h, a = divmod(u, BLOCKS)
             dst = out_1[a].rearrange("p t i -> p (t i)")[:, 4 * HALF * h : 4 * HALF * (h + 1)]
@@ -196,74 +200,116 @@ def tile_mix_outl_fm_pl_relu2_kernel(tc, x, w8_words, w8_scales, w4_words, w4_sc
         load_w4(0, 1)
         load_x(1, 0, QUARTER)
         load_scales(nc.sync, w4_scales, 0)
-        load_x(0, QUARTER, QUARTER)
         load_w8(1, 1)
-        load_x(1, QUARTER, QUARTER)
         load_w4(1, 1)
+        load_x(0, QUARTER, QUARTER)
+        load_x(1, QUARTER, QUARTER)
         load_w8(2, 2)
         load_w4(2, 2)
         load_x(0, HALF, HALF)
         load_x(1, HALF, HALF)
 
-        new_result(0)
+        def vector_bank(u, r):
+            if u < UNITS and r < VECTOR_BANKS[u]:
+                multiply(u, r)
+                relu_vector(u, r)
+
+        def deal(a):
+            deal_w8(a)
+            deal_w4(a)
+            deal_scales(a)
+
+        for u in range(3):
+            new_result(u)
         round_x(True, 0, 0)
         deal_w8(0)
         deal_w4(0)
         quantize_x(0, 0)
         round_x(False, 1, 0)
         deal_scales(0)
-        first_w8(0)
         quantize_x(1, 0)
-        first_w4(0)
-        round_x(True, 0, QUARTER)
+        quarter_bank(0, 0, 0, True)
+        quarter_bank(0, 0, 1, True)
+        deal(1)
+        quarter_bank(1, 0, 0, True)
+        quarter_square(0, 0)
+        quarter_bank(1, 0, 1, True)
+        round_x(False, 0, QUARTER)
         round_x(False, 1, QUARTER)
         quantize_x(0, QUARTER)
-        first_w8(1)
-        deal_w8(1)
+        deal_w8(2)
         quantize_x(1, QUARTER)
-        first_w4(1)
-        first_epilogue(0)
-        first_epilogue(1)
-        store_result(0, 0)
-        store_result(0, 2)
-        deal_w4(1)
-        deal_scales(1)
-        for a in (2, 3):
-            deal_w8(a)
-            deal_w4(a)
-            deal_scales(a)
+        quarter_square(1, 0)
+        quarter_bank(0, 1, 0, True)
+        deal_w4(2)
+        deal_scales(2)
+        quarter_bank(0, 1, 1, False)
+        quarter_bank(1, 1, 0, True)
+        quarter_square(0, 1)
+        deal_w8(3)
+        quarter_bank(1, 1, 1, False)
+        quarter_square(1, 1)
+        deal_w4(3)
+        deal_scales(3)
+        round_x(False, 0, HALF)
+        round_result(0)
+        vector_bank(2, 0)
+        quantize_x(0, HALF)
+        vector_bank(2, 1)
+        quantize_result(0)
+        store_words(0)
 
-        def extra(u, slot):
-            if u == 1 and slot == 0:
-                round_x(False, 0, HALF)
-            if u == 1 and slot == 1:
-                round_x(False, 1, HALF)
-                quantize_x(0, HALF)
-            if u == 2 and slot == 0:
-                quantize_x(1, HALF)
-            if u + 1 < UNITS and slot < VECTOR_BANKS[u + 1]:
-                multiply(u + 1, slot)
-                relu_vector(u + 1, slot)
-
-        new_result(1)
-        for u in range(1, UNITS):
-            if u + 1 < UNITS:
-                new_result(u + 1)
+        last = UNITS - 1
+        for u in range(2, last):
+            new_result(u + 1)
             for r in range(VECTOR_BANKS[u], 4):
                 multiply(u, r)
                 relu_scalar(u, r)
             round_result(u - 1)
-            extra(u, 0)
+            if u == 2:
+                round_x(False, 1, HALF)
+            vector_bank(u + 1, 0)
+            vector_bank(u + 1, 1)
             quantize_result(u - 1)
-            extra(u, 1)
+            if u == 2:
+                quantize_x(1, HALF)
+            vector_bank(u + 1, 2)
+
             square(u, 0)
             store_result(u, 0)
-            store_words(u - 1)
             square(u, 2)
             store_result(u, 2)
-        round_result(UNITS - 1)
-        quantize_result(UNITS - 1)
-        store_words(UNITS - 1)
+            store_words(u - 1)
+
+        multiply(last, 3)
+        relu_vector(last, 3)
+        square(last, 0)
+        store_result(last, 0)
+        multiply(last, 2)
+        relu_scalar(last, 2)
+        round_result(last - 1)
+        square_cols(last, 3, 0, HALF)
+        store_result(last, 3, 1)
+        quantize_result(last - 1)
+        store_words(last - 1)
+        square_cols(last, 2, 0, QUARTER)
+        square_cols(last, 2, QUARTER, QUARTER)
+        store_result(last, 2, 1)
+        h, a = divmod(last, BLOCKS)
+        tail_bf = [sbuf("tail_bf_%d" % c, [P, 4 * QUARTER], BF16) for c in range(2)]
+        tail_words = [sbuf("tail_words_%d" % c, [P, QUARTER], U32) for c in range(2)]
+        interleave(False, tail_bf[0][:], result[last][:, :, 0:QUARTER])
+        interleave(True, tail_bf[1][:, 4 * P : 8 * P], result[last][:, :, QUARTER + P : HALF])
+        interleave(False, tail_bf[1][:, 0 : 4 * P], result[last][:, :, QUARTER : QUARTER + P])
+        for c in range(2):
+            t0 = HALF * h + QUARTER * c
+            nc.vector.quantize_mx(
+                out=tail_words[c][:].bitcast(FP8X4),
+                scales=out_scales[4 * a : P, t0 : t0 + QUARTER],
+                in_=tail_bf[c][:],
+            )
+            dst = out_1[a].rearrange("p t i -> p (t i)")[:, 4 * t0 : 4 * (t0 + QUARTER)]
+            nc.sync.dma_start(out=dst.bitcast(I32), in_=tail_words[c][:].bitcast(I32))
         for q in range(4):
             queue = nc.sync if q % 2 else nc.scalar
             queue.dma_start(out=out_2[:, 4 * q : 4 * q + 4, :].bitcast(I32), in_=out_scales[32 * q : 32 * q + 16, :].bitcast(I32))

@@ -21,6 +21,7 @@ QUARTER = 256
 BLOCKS = 4
 UNITS = 8
 VECTOR_BANKS = [0,0,0,1,2,2,2,2]
+ROUNDINGS = [0,0,1,2,1,1,1]
 
 
 def tile_mix_outl_fm_pl_relu2_kernel(tc, x, w8_words, w8_scales, w4_words, w4_scales, out_0, out_1, out_2):
@@ -41,7 +42,10 @@ def tile_mix_outl_fm_pl_relu2_kernel(tc, x, w8_words, w8_scales, w4_words, w4_sc
         x_codes = {(g, h): sbuf("x_codes_%d_%d" % (g, h), [P, HALF], U32) for g in range(2) for h in range(2)}
         x_scales = {(g, h): sbuf("x_scales_%d_%d" % (g, h), [P, HALF], U8) for g in range(2) for h in range(2)}
         x_raw, x_bf, w8_raw, w4_raw, w8, w4, w_scales = {}, {}, {}, {}, {}, {}, {}
-        banks, result, result_bf, words = {}, {}, {}, {}
+        result_bf = {}
+        banks_used = []
+        result = [sbuf("result_%d" % a, [P, 4, T], F32) for a in range(BLOCKS)]
+        words = [sbuf("words_%d" % a, [P, T], U32) for a in range(BLOCKS)]
 
         def load_x(g, t0, width):
             x_raw[g, t0] = sbuf("x_raw_%d_%d" % (g, t0), [P, 4, width], F32)
@@ -60,9 +64,9 @@ def tile_mix_outl_fm_pl_relu2_kernel(tc, x, w8_words, w8_scales, w4_words, w4_sc
                 w4_raw[a + i] = raw[:, 1024 * i : 1024 * (i + 1)]
 
         def load_scales(queue, scales, first_row):
-            for q in range(4):
-                row = 32 * q + first_row
-                queue.dma_start(out=scale_raw[row : row + 4, :].bitcast(I32), in_=scales[0, 4 * q : 4 * q + 4, :].bitcast(I32))
+            rows = scales[0].rearrange("(q r) n -> r q n", r=4)
+            for r in range(4):
+                queue.dma_start(out=scale_raw[first_row + r : P : 32, :].bitcast(I32), in_=rows[r].bitcast(I32))
 
         def deal_w8(a):
             w8[a] = sbuf("w8_%d" % a, [P, 512], U32)
@@ -86,8 +90,8 @@ def tile_mix_outl_fm_pl_relu2_kernel(tc, x, w8_words, w8_scales, w4_words, w4_sc
             )
 
         def interleave(on_scalar, dst, src):
-            out = dst.rearrange("p (c i j) -> p c j i", i=4, j=4)
-            in_ = src.rearrange("p j (c i) -> p c j i", i=4)
+            out = dst.rearrange("p (c i j) -> p c j i", i=2, j=4)
+            in_ = src.rearrange("p j (c i) -> p c j i", i=2)
             if on_scalar:
                 nc.scalar.activation(out=out, in_=in_, func=ACT.Copy)
             else:
@@ -129,69 +133,62 @@ def tile_mix_outl_fm_pl_relu2_kernel(tc, x, w8_words, w8_scales, w4_words, w4_sc
                 stop=stop,
             )
 
+        def next_bank(shape):
+            n = len(banks_used)
+            banks_used.append(n)
+            return psum.tile(shape, F32, name="acc_%d" % n, tag="bank%d" % (n % 8))
+
+        def relu(on_scalar, out, bank):
+            if on_scalar:
+                nc.scalar.activation(out=out, in_=bank, func=ACT.Relu)
+            else:
+                nc.vector.tensor_scalar_max(out=out, in0=bank, scalar1=0.0)
+
         def quarter_bank(a, c, b, on_scalar):
-            bank = psum.tile([P, 2, QUARTER], F32, name="q_%d_%d_%d" % (a, c, b), tag="bank%d" % (4 * c + 2 * a + b))
+            bank = next_bank([P, 2, QUARTER])
             for i in range(2):
                 pass_w8(bank[:, i, :], a, 2 * b + i, 0, QUARTER * c, QUARTER, i == 0)
             for i in range(2):
                 for n in range(2):
                     pass_w4(bank[:, i, P * n : P * (n + 1)], a, 2 * b + i, 0, QUARTER * c + P * n, P, i == 1 and n == 1)
-            out = result[a][:, 2 * b : 2 * b + 2, QUARTER * c : QUARTER * (c + 1)]
-            if on_scalar:
-                nc.scalar.activation(out=out, in_=bank[:], func=ACT.Relu)
-            else:
-                nc.vector.tensor_scalar_max(out=out, in0=bank[:], scalar1=0.0)
+            relu(on_scalar, result[a][:, 2 * b : 2 * b + 2, QUARTER * c : QUARTER * (c + 1)], bank[:])
 
-        def quarter_square(a, c):
-            part = result[a][:, :, QUARTER * c : QUARTER * (c + 1)]
+        def half_bank(a, r, h, on_scalar):
+            bank = next_bank([P, HALF])
+            pass_w8(bank[:], a, r, h, 0, HALF, True)
+            pass_w4(bank[:], a, r, h, 0, HALF, True)
+            relu(on_scalar, result[a][:, r, HALF * h : HALF * (h + 1)], bank[:])
+
+        def square(a, r0, rows, t0, width):
+            part = result[a][:, r0 : r0 + rows, t0 : t0 + width]
             nc.scalar.activation(out=part, in_=part, func=ACT.Square)
-            store_result(a, 0, 4, QUARTER * c, QUARTER)
 
-        def multiply(u, r):
-            h, a = divmod(u, BLOCKS)
-            banks[u, r] = psum.tile([P, HALF], F32, name="acc_%d_%d" % (u, r), tag="bank%d" % (4 * (u % 2) + r))
-            pass_w8(banks[u, r][:], a, r, h, 0, HALF, True)
-            pass_w4(banks[u, r][:], a, r, h, 0, HALF, True)
+        def store_result(a, r0, rows, t0, width):
+            dst = out_0[512 * a : 512 * (a + 1), t0 : t0 + width].rearrange("(p r) t -> p r t", r=4)
+            nc.sync.dma_start(out=dst[:, r0 : r0 + rows, :], in_=result[a][:, r0 : r0 + rows, t0 : t0 + width])
 
-        def new_result(u):
-            result[u] = sbuf("result_%d" % u, [P, 4, HALF], F32)
+        def round_result(a, h):
+            result_bf[a, h] = sb.tile([P, 4 * HALF], BF16, name="result_bf_%d_%d" % (a, h), tag="result_bf", bufs=2, align_bytes=64)
+            interleave(False, result_bf[a, h][:], result[a][:, :, HALF * h : HALF * (h + 1)])
 
-        def relu_vector(u, r):
-            nc.vector.tensor_scalar_max(out=result[u][:, r, :], in0=banks[u, r][:], scalar1=0.0)
-
-        def relu_scalar(u, r):
-            nc.scalar.activation(out=result[u][:, r, :], in_=banks[u, r][:], func=ACT.Relu)
-
-        def square(u, r0):
-            rows = result[u][:, r0 : r0 + 2, :]
-            nc.scalar.activation(out=rows, in_=rows, func=ACT.Square)
-
-        def store_result(u, r0, rows=2, c0=0, width=HALF):
-            h, a = divmod(u, BLOCKS)
-            dst = out_0[512 * a : 512 * (a + 1), HALF * h + c0 : HALF * h + c0 + width].rearrange("(p r) t -> p r t", r=4)
-            nc.sync.dma_start(out=dst[:, r0 : r0 + rows, :], in_=result[u][:, r0 : r0 + rows, c0 : c0 + width])
-
-        def round_result(u):
-            result_bf[u] = sb.tile([P, 4 * HALF], BF16, name="result_bf_%d" % u, tag="result_bf", bufs=2, align_bytes=64)
-            interleave(False, result_bf[u][:], result[u][:])
-
-        def quantize_result(u):
-            h, a = divmod(u, BLOCKS)
-            words[u] = sbuf("words_%d" % u, [P, HALF], U32)
+        def quantize_part(a, t0, width, src):
             nc.vector.quantize_mx(
-                out=words[u][:].bitcast(FP8X4),
-                scales=out_scales[4 * a : P, HALF * h : HALF * (h + 1)],
-                in_=result_bf[u][:],
+                out=words[a][:, t0 : t0 + width].bitcast(FP8X4),
+                scales=out_scales[4 * a : P, t0 : t0 + width],
+                in_=src,
             )
 
-        def square_cols(u, r, c0, width):
-            rows = result[u][:, r, c0 : c0 + width]
-            nc.scalar.activation(out=rows, in_=rows, func=ACT.Square)
+        def quantize_result(a, h):
+            quantize_part(a, HALF * h, HALF, result_bf[a, h][:])
 
-        def store_words(u):
-            h, a = divmod(u, BLOCKS)
-            dst = out_1[a].rearrange("p t i -> p (t i)")[:, 4 * HALF * h : 4 * HALF * (h + 1)]
-            nc.sync.dma_start(out=dst.bitcast(I32), in_=words[u][:].bitcast(I32))
+        def store_words(a, t0, width):
+            dst = out_1[a].rearrange("p t i -> p (t i)")[:, 4 * t0 : 4 * (t0 + width)]
+            nc.sync.dma_start(out=dst.bitcast(I32), in_=words[a][:, t0 : t0 + width].bitcast(I32))
+
+        def deal(a):
+            deal_w8(a)
+            deal_w4(a)
+            deal_scales(a)
 
         nc.vector.memset(scale_raw[:].bitcast(I32), 0)
         load_x(0, 0, QUARTER)
@@ -209,18 +206,6 @@ def tile_mix_outl_fm_pl_relu2_kernel(tc, x, w8_words, w8_scales, w4_words, w4_sc
         load_x(0, HALF, HALF)
         load_x(1, HALF, HALF)
 
-        def vector_bank(u, r):
-            if u < UNITS and r < VECTOR_BANKS[u]:
-                multiply(u, r)
-                relu_vector(u, r)
-
-        def deal(a):
-            deal_w8(a)
-            deal_w4(a)
-            deal_scales(a)
-
-        for u in range(3):
-            new_result(u)
         round_x(True, 0, 0)
         deal_w8(0)
         deal_w4(0)
@@ -232,84 +217,88 @@ def tile_mix_outl_fm_pl_relu2_kernel(tc, x, w8_words, w8_scales, w4_words, w4_sc
         quarter_bank(0, 0, 1, True)
         deal(1)
         quarter_bank(1, 0, 0, True)
-        quarter_square(0, 0)
+        square(0, 0, 4, 0, QUARTER)
         quarter_bank(1, 0, 1, True)
         round_x(False, 0, QUARTER)
         round_x(False, 1, QUARTER)
         quantize_x(0, QUARTER)
-        deal_w8(2)
         quantize_x(1, QUARTER)
-        quarter_square(1, 0)
+        square(1, 0, 4, 0, QUARTER)
         quarter_bank(0, 1, 0, True)
-        deal_w4(2)
-        deal_scales(2)
+        deal(2)
         quarter_bank(0, 1, 1, False)
         quarter_bank(1, 1, 0, True)
-        quarter_square(0, 1)
-        deal_w8(3)
+        square(0, 0, 4, QUARTER, QUARTER)
+        store_result(0, 0, 4, 0, HALF)
         quarter_bank(1, 1, 1, False)
-        quarter_square(1, 1)
-        deal_w4(3)
-        deal_scales(3)
-        round_x(False, 0, HALF)
-        round_result(0)
-        vector_bank(2, 0)
-        quantize_x(0, HALF)
-        vector_bank(2, 1)
-        quantize_result(0)
-        store_words(0)
+        for r in range(VECTOR_BANKS[2]):
+            half_bank(2, r, 0, False)
+        square(1, 0, 4, QUARTER, QUARTER)
+        store_result(1, 0, 4, 0, HALF)
+        deal(3)
 
+        done = []
         last = UNITS - 1
         for u in range(2, last):
-            new_result(u + 1)
+            h, a = divmod(u, BLOCKS)
+            nh, na = divmod(u + 1, BLOCKS)
             for r in range(VECTOR_BANKS[u], 4):
-                multiply(u, r)
-                relu_scalar(u, r)
-            round_result(u - 1)
+                half_bank(a, r, h, True)
+            fillers = [(na, r, nh) for r in range(VECTOR_BANKS[u + 1])]
             if u == 2:
+                round_x(False, 0, HALF)
+                for job in fillers:
+                    half_bank(*job, False)
+                fillers = []
                 round_x(False, 1, HALF)
-            vector_bank(u + 1, 0)
-            vector_bank(u + 1, 1)
-            quantize_result(u - 1)
-            if u == 2:
+                quantize_x(0, HALF)
+            stores = []
+            for n in range(ROUNDINGS[u]):
+                ph, pa = divmod(len(done), BLOCKS)
+                done.append(pa)
+                round_result(pa, ph)
+                if u == 2:
+                    quantize_x(1, HALF)
+                if fillers:
+                    half_bank(*fillers.pop(0), False)
+                if len(fillers) > ROUNDINGS[u] - n - 1:
+                    half_bank(*fillers.pop(0), False)
+                quantize_result(pa, ph)
+                stores.append((pa, ph))
+            if u == 2 and not ROUNDINGS[u]:
                 quantize_x(1, HALF)
-            vector_bank(u + 1, 2)
+            for job in fillers:
+                half_bank(*job, False)
+            square(a, 0, 2, HALF * h, HALF)
+            store_result(a, 0, 2, HALF * h, HALF)
+            square(a, 2, 2, HALF * h, HALF)
+            store_result(a, 2, 2, HALF * h, HALF)
+            for pa, ph in stores:
+                store_words(pa, HALF * ph, HALF)
 
-            square(u, 0)
-            store_result(u, 0)
-            square(u, 2)
-            store_result(u, 2)
-            store_words(u - 1)
-
-        multiply(last, 3)
-        relu_vector(last, 3)
-        square(last, 0)
-        store_result(last, 0)
-        multiply(last, 2)
-        relu_scalar(last, 2)
-        round_result(last - 1)
-        square_cols(last, 3, 0, HALF)
-        store_result(last, 3, 1)
-        quantize_result(last - 1)
-        store_words(last - 1)
-        square_cols(last, 2, 0, QUARTER)
-        square_cols(last, 2, QUARTER, QUARTER)
-        store_result(last, 2, 1)
-        h, a = divmod(last, BLOCKS)
+        a = BLOCKS - 1
+        assert VECTOR_BANKS[last] in (1, 2)
+        for r in range(VECTOR_BANKS[last], 2):
+            half_bank(a, r, 1, True)
+        half_bank(a, 2, 1, True)
+        square(a, 0, 2, HALF, HALF)
+        store_result(a, 0, 2, HALF, HALF)
+        half_bank(a, 3, 1, True)
+        for n in range(len(done), last):
+            ph, pa = divmod(n, BLOCKS)
+            round_result(pa, ph)
+            quantize_result(pa, ph)
+            store_words(pa, HALF * ph, HALF)
+        square(a, 2, 2, HALF, QUARTER)
+        square(a, 2, 2, HALF + QUARTER, QUARTER)
+        store_result(a, 2, 2, HALF, HALF)
         tail_bf = [sbuf("tail_bf_%d" % c, [P, 4 * QUARTER], BF16) for c in range(2)]
-        tail_words = [sbuf("tail_words_%d" % c, [P, QUARTER], U32) for c in range(2)]
-        interleave(False, tail_bf[0][:], result[last][:, :, 0:QUARTER])
-        interleave(True, tail_bf[1][:, 4 * P : 8 * P], result[last][:, :, QUARTER + P : HALF])
-        interleave(False, tail_bf[1][:, 0 : 4 * P], result[last][:, :, QUARTER : QUARTER + P])
+        interleave(False, tail_bf[0][:], result[a][:, :, HALF : HALF + QUARTER])
+        interleave(True, tail_bf[1][:, 4 * P : 8 * P], result[a][:, :, HALF + QUARTER + P : T])
+        interleave(False, tail_bf[1][:, 0 : 4 * P], result[a][:, :, HALF + QUARTER : HALF + QUARTER + P])
         for c in range(2):
-            t0 = HALF * h + QUARTER * c
-            nc.vector.quantize_mx(
-                out=tail_words[c][:].bitcast(FP8X4),
-                scales=out_scales[4 * a : P, t0 : t0 + QUARTER],
-                in_=tail_bf[c][:],
-            )
-            dst = out_1[a].rearrange("p t i -> p (t i)")[:, 4 * t0 : 4 * (t0 + QUARTER)]
-            nc.sync.dma_start(out=dst.bitcast(I32), in_=tail_words[c][:].bitcast(I32))
+            quantize_part(a, HALF + QUARTER * c, QUARTER, tail_bf[c][:])
+        store_words(a, HALF, HALF)
         for q in range(4):
             queue = nc.sync if q % 2 else nc.scalar
             queue.dma_start(out=out_2[:, 4 * q : 4 * q + 4, :].bitcast(I32), in_=out_scales[32 * q : 32 * q + 16, :].bitcast(I32))

from contextlib import ExitStack

import concourse.mybir as mybir

K, M, T = 1024, 2048, 1024
FLOPS = 2 * K * M * T

F32 = mybir.dt.float32
BF16 = mybir.dt.bfloat16
I32 = mybir.dt.int32
U32 = mybir.dt.uint32
U8 = mybir.dt.uint8
FP8X4 = mybir.dt.float8_e4m3fn_x4
FP4X4 = mybir.dt.float4_e2m1fn_x4
ACT = mybir.ActivationFunctionType
ALU = mybir.AluOpType

P = 128
HALF = 512
QUARTER = 256
BLOCKS = 4
UNITS = 8
VECTOR_BANKS = [0,0,0,1,2,2,2,2]
ROUNDINGS = [0,0,1,2,1,1,1]


def tile_mix_outl_fm_pl_relu2_kernel(tc, x, w8_words, w8_scales, w4_words, w4_scales, out_0, out_1, out_2):
    nc = tc.nc
    w8_bytes = w8_words[0].rearrange("p n i -> p (n i)")
    w4_bytes = w4_words[0]

    with ExitStack() as ctx:
        sb = ctx.enter_context(tc.tile_pool(name="sb", bufs=1))
        psum = ctx.enter_context(tc.psum_pool(name="psum", bufs=1))
        ctx.enter_context(tc.manual_schedule())

        def sbuf(name, shape, dtype):
            return sb.tile(shape, dtype, name=name, align_bytes=64)

        scale_raw = sbuf("scale_raw", [P, M], U8)
        out_scales = sbuf("out_scales", [P, T], U8)
        x_codes = {(g, h): sbuf("x_codes_%d_%d" % (g, h), [P, HALF], U32) for g in range(2) for h in range(2)}
        x_scales = {(g, h): sbuf("x_scales_%d_%d" % (g, h), [P, HALF], U8) for g in range(2) for h in range(2)}
        x_raw, x_bf, w8_raw, w4_raw, w8, w4, w_scales = {}, {}, {}, {}, {}, {}, {}
        result_bf = {}
        banks_used = []
        result = [sbuf("result_%d" % a, [P, 4, T], F32) for a in range(BLOCKS)]
        words = [sbuf("words_%d" % a, [P, T], U32) for a in range(BLOCKS)]

        def load_x(g, t0, width):
            x_raw[g, t0] = sbuf("x_raw_%d_%d" % (g, t0), [P, 4, width], F32)
            nc.sync.dma_start(out=x_raw[g, t0][:], in_=x[512 * g : 512 * (g + 1), t0 : t0 + width].rearrange("(p j) w -> p j w", j=4))

        def load_w8(a, count):
            raw = sbuf("w8_raw_%d" % a, [P, 512 * count], I32)
            nc.sync.dma_start(out=raw[:], in_=w8_bytes[:, 2048 * a : 2048 * (a + count)].bitcast(I32))
            for i in range(count):
                w8_raw[a + i] = raw[:, 512 * i : 512 * (i + 1)]

        def load_w4(a, count):
            raw = sbuf("w4_raw_%d" % a, [P, 1024 * count], U8)
            nc.sync.dma_start(out=raw[:].bitcast(I32), in_=w4_bytes[:, 1024 * a : 1024 * (a + count)].bitcast(I32))
            for i in range(count):
                w4_raw[a + i] = raw[:, 1024 * i : 1024 * (i + 1)]

        def load_scales(queue, scales, first_row):
            rows = scales[0].rearrange("(q r) n -> r q n", r=4)
            for r in range(4):
                queue.dma_start(out=scale_raw[first_row + r : P : 32, :].bitcast(I32), in_=rows[r].bitcast(I32))

        def deal_w8(a):
            w8[a] = sbuf("w8_%d" % a, [P, 512], U32)
            nc.vector.tensor_copy(
                out=w8[a][:].bitcast(I32).rearrange("p (r h l) -> p h r l", r=4, l=4),
                in_=w8_raw[a].rearrange("p (h l r) -> p h r l", r=4, l=4),
            )

        def deal_w4(a):
            w4[a] = sbuf("w4_%d" % a, [P, 1024], U8)
            nc.vector.tensor_copy(
                out=w4[a][:].rearrange("p (r h l b) -> p h r l b", r=4, l=8, b=2),
                in_=w4_raw[a].rearrange("p (h l r b) -> p h r l b", r=4, l=8, b=2),
            )

        def deal_scales(a):
            w_scales[a] = sbuf("w_scales_%d" % a, [P, 512], U8)
            nc.vector.tensor_copy(
                out=w_scales[a][:].rearrange("p (r h l) -> p h r l", r=4, l=16),
                in_=scale_raw[:, 512 * a : 512 * (a + 1)].rearrange("p (h l r) -> p h r l", r=4, l=16),
            )

        def interleave(on_scalar, dst, src):
            out = dst.rearrange("p (c i j) -> p c j i", i=2, j=4)
            in_ = src.rearrange("p j (c i) -> p c j i", i=2)
            if on_scalar:
                nc.scalar.activation(out=out, in_=in_, func=ACT.Copy)
            else:
                nc.vector.tensor_copy(out=out, in_=in_)

        def round_x(on_scalar, g, t0):
            width = x_raw[g, t0].shape[2]
            x_bf[g, t0] = sbuf("x_bf_%d_%d" % (g, t0), [P, 4 * width], BF16)
            interleave(on_scalar, x_bf[g, t0][:], x_raw[g, t0][:])

        def quantize_x(g, t0):
            width = x_raw[g, t0].shape[2]
            h, c0 = divmod(t0, HALF)
            nc.vector.quantize_mx(
                out=x_codes[g, h][:, c0 : c0 + width].bitcast(FP8X4),
                scales=x_scales[g, h][:, c0 : c0 + width],
                in_=x_bf[g, t0][:],
            )

        def pass_w8(out, a, r, h, c0, width, start):
            nc.tensor.matmul_mx(
                out=out,
                lhsT=w8[a][:, P * r : P * (r + 1)].bitcast(FP8X4),
                lhsT_scale=w_scales[a][4:P, P * r : P * (r + 1)],
                rhs=x_codes[0, h][:, c0 : c0 + width].bitcast(FP8X4),
                rhs_scale=x_scales[0, h][:, c0 : c0 + width],
                start=start,
                stop=False,
            )

        def pass_w4(out, a, r, h, c0, width, stop):
            nc.tensor.matmul_mx(
                out=out,
                lhsT=w4[a][:, 2 * P * r : 2 * P * (r + 1)].bitcast(FP4X4),
                lhsT_scale=w_scales[a][:, P * r : P * (r + 1)],
                rhs=x_codes[1, h][:, c0 : c0 + width].bitcast(FP8X4),
                rhs_scale=x_scales[1, h][:, c0 : c0 + width],
                start=False,
                stop=stop,
            )

        def next_bank(shape):
            n = len(banks_used)
            banks_used.append(n)
            return psum.tile(shape, F32, name="acc_%d" % n, tag="bank%d" % (n % 8))

        def relu(on_scalar, out, bank):
            if on_scalar:
                nc.scalar.activation(out=out, in_=bank, func=ACT.Relu)
            else:
                nc.vector.tensor_scalar_max(out=out, in0=bank, scalar1=0.0)

        def quarter_bank(a, c, b, on_scalar):
            bank = next_bank([P, 2, QUARTER])
            for i in range(2):
                pass_w8(bank[:, i, :], a, 2 * b + i, 0, QUARTER * c, QUARTER, i == 0)
            for i in range(2):
                for n in range(2):
                    pass_w4(bank[:, i, P * n : P * (n + 1)], a, 2 * b + i, 0, QUARTER * c + P * n, P, i == 1 and n == 1)
            relu(on_scalar, result[a][:, 2 * b : 2 * b + 2, QUARTER * c : QUARTER * (c + 1)], bank[:])

        def half_bank(a, r, h, on_scalar):
            bank = next_bank([P, HALF])
            pass_w8(bank[:], a, r, h, 0, HALF, True)
            pass_w4(bank[:], a, r, h, 0, HALF, True)
            relu(on_scalar, result[a][:, r, HALF * h : HALF * (h + 1)], bank[:])

        def square(a, r0, rows, t0, width):
            part = result[a][:, r0 : r0 + rows, t0 : t0 + width]
            nc.scalar.activation(out=part, in_=part, func=ACT.Square)

        def store_result(a, r0, rows, t0, width):
            dst = out_0[512 * a : 512 * (a + 1), t0 : t0 + width].rearrange("(p r) t -> p r t", r=4)
            nc.sync.dma_start(out=dst[:, r0 : r0 + rows, :], in_=result[a][:, r0 : r0 + rows, t0 : t0 + width])

        def round_result(a, h):
            result_bf[a, h] = sb.tile([P, 4 * HALF], BF16, name="result_bf_%d_%d" % (a, h), tag="result_bf", bufs=2, align_bytes=64)
            interleave(False, result_bf[a, h][:], result[a][:, :, HALF * h : HALF * (h + 1)])

        def quantize_part(a, t0, width, src):
            nc.vector.quantize_mx(
                out=words[a][:, t0 : t0 + width].bitcast(FP8X4),
                scales=out_scales[4 * a : P, t0 : t0 + width],
                in_=src,
            )

        def quantize_result(a, h):
            quantize_part(a, HALF * h, HALF, result_bf[a, h][:])

        def store_words(a, t0, width):
            dst = out_1[a].rearrange("p t i -> p (t i)")[:, 4 * t0 : 4 * (t0 + width)]
            nc.sync.dma_start(out=dst.bitcast(I32), in_=words[a][:, t0 : t0 + width].bitcast(I32))

        def deal(a):
            deal_w8(a)
            deal_w4(a)
            deal_scales(a)

        nc.vector.memset(scale_raw[:].bitcast(I32), 0)
        load_x(0, 0, QUARTER)
        load_scales(nc.sync, w8_scales, 4)
        load_w8(0, 1)
        load_w4(0, 1)
        load_x(1, 0, QUARTER)
        load_scales(nc.sync, w4_scales, 0)
        load_w8(1, 1)
        load_w4(1, 1)
        load_x(0, QUARTER, QUARTER)
        load_x(1, QUARTER, QUARTER)
        load_w8(2, 2)
        load_w4(2, 2)
        load_x(0, HALF, HALF)
        load_x(1, HALF, HALF)

        round_x(True, 0, 0)
        deal_w8(0)
        deal_w4(0)
        quantize_x(0, 0)
        round_x(False, 1, 0)
        deal_scales(0)
        quantize_x(1, 0)
        quarter_bank(0, 0, 0, True)
        quarter_bank(0, 0, 1, True)
        deal(1)
        quarter_bank(1, 0, 0, True)
        square(0, 0, 4, 0, QUARTER)
        quarter_bank(1, 0, 1, True)
        round_x(False, 0, QUARTER)
        round_x(False, 1, QUARTER)
        quantize_x(0, QUARTER)
        quantize_x(1, QUARTER)
        square(1, 0, 4, 0, QUARTER)
        quarter_bank(0, 1, 0, True)
        deal(2)
        quarter_bank(0, 1, 1, False)
        quarter_bank(1, 1, 0, True)
        square(0, 0, 4, QUARTER, QUARTER)
        store_result(0, 0, 4, 0, HALF)
        quarter_bank(1, 1, 1, False)
        for r in range(VECTOR_BANKS[2]):
            half_bank(2, r, 0, False)
        square(1, 0, 4, QUARTER, QUARTER)
        store_result(1, 0, 4, 0, HALF)
        deal(3)

        done = []
        last = UNITS - 1
        for u in range(2, last):
            h, a = divmod(u, BLOCKS)
            nh, na = divmod(u + 1, BLOCKS)
            for r in range(VECTOR_BANKS[u], 4):
                half_bank(a, r, h, True)
            fillers = [(na, r, nh) for r in range(VECTOR_BANKS[u + 1])]
            if u == 2:
                round_x(False, 0, HALF)
                for job in fillers:
                    half_bank(*job, False)
                fillers = []
                round_x(False, 1, HALF)
                quantize_x(0, HALF)
            stores = []
            for n in range(ROUNDINGS[u]):
                ph, pa = divmod(len(done), BLOCKS)
                done.append(pa)
                round_result(pa, ph)
                if u == 2:
                    quantize_x(1, HALF)
                if fillers:
                    half_bank(*fillers.pop(0), False)
                if len(fillers) > ROUNDINGS[u] - n - 1:
                    half_bank(*fillers.pop(0), False)
                quantize_result(pa, ph)
                stores.append((pa, ph))
            if u == 2 and not ROUNDINGS[u]:
                quantize_x(1, HALF)
            for job in fillers:
                half_bank(*job, False)
            square(a, 0, 2, HALF * h, HALF)
            store_result(a, 0, 2, HALF * h, HALF)
            square(a, 2, 2, HALF * h, HALF)
            store_result(a, 2, 2, HALF * h, HALF)
            for pa, ph in stores:
                store_words(pa, HALF * ph, HALF)

        a = BLOCKS - 1
        assert VECTOR_BANKS[last] in (1, 2)
        for r in range(VECTOR_BANKS[last], 2):
            half_bank(a, r, 1, True)
        half_bank(a, 2, 1, True)
        square(a, 0, 2, HALF, HALF)
        store_result(a, 0, 2, HALF, HALF)
        half_bank(a, 3, 1, True)
        for n in range(len(done), last):
            ph, pa = divmod(n, BLOCKS)
            round_result(pa, ph)
            quantize_result(pa, ph)
            store_words(pa, HALF * ph, HALF)
        square(a, 2, 2, HALF, QUARTER)
        square(a, 2, 2, HALF + QUARTER, QUARTER)
        store_result(a, 2, 2, HALF, HALF)
        tail_bf = [sbuf("tail_bf_%d" % c, [P, 4 * QUARTER], BF16) for c in range(2)]
        interleave(False, tail_bf[0][:], result[a][:, :, HALF : HALF + QUARTER])
        interleave(True, tail_bf[1][:, 4 * P : 8 * P], result[a][:, :, HALF + QUARTER + P : T])
        interleave(False, tail_bf[1][:, 0 : 4 * P], result[a][:, :, HALF + QUARTER : HALF + QUARTER + P])
        for c in range(2):
            quantize_part(a, HALF + QUARTER * c, QUARTER, tail_bf[c][:])
        store_words(a, HALF, HALF)
        for q in range(4):
            queue = nc.sync if q % 2 else nc.scalar
            queue.dma_start(out=out_2[:, 4 * q : 4 * q + 4, :].bitcast(I32), in_=out_scales[32 * q : 32 * q + 16, :].bitcast(I32))
